import numpy as np
import ml_dtypes


def mxq(x, axis, fmt="e4m3"):
    dtype, down = {"e4m3": (ml_dtypes.float8_e4m3fn, 7), "e5m2": (ml_dtypes.float8_e5m2, 14)}[fmt]
    v = np.moveaxis(np.asarray(x, np.float32).astype(ml_dtypes.bfloat16).astype(np.float64), axis, -1)
    blocks = v.reshape(v.shape[:-1] + (-1, 32))
    amax = np.abs(blocks).max(-1, keepdims=True)
    byte = np.maximum(np.where(amax > 0, np.frexp(amax)[1] - 1 + 127, 0) - down, 1)
    scale = np.exp2(byte - 127.0)
    codes = (blocks / scale).astype(np.float32).astype(dtype).astype(np.float64)
    return np.moveaxis((codes * scale).reshape(v.shape), -1, axis)


WIDE = False


def mx_kscale(k):
    if not WIDE:
        return np.ones(k)
    levels = np.array([10, -10, 5, -5, 0])
    if k % 512:
        return np.exp2(np.random.permutation(np.resize(levels, k // 32))).repeat(32)
    a = np.empty((k // 512, 16))
    for p in range(k // 512):
        a[p, :8] = np.random.permutation(np.resize(levels, 8))
        for g in range(8):
            far = levels[np.abs(levels - a[p, g]) >= 10]
            a[p, g + 8] = far[np.random.randint(len(far))]
    return np.exp2(a.ravel()).repeat(32)


def f64(x):
    return np.asarray(x).astype(np.float64)


def striped(idx):
    return np.tile(idx.reshape(-1, 16).T, (8, 1)).astype(np.uint16)


def unstriped(offs):
    return offs[:16].T.reshape(-1).astype(np.int64)


def pack_weight(w):
    k, n = w.shape
    w = f64(np.asarray(w, np.float32).astype(ml_dtypes.bfloat16)).reshape(k // 32, 32, n)
    amax = np.abs(w).max(1)
    byte = np.clip(np.where(amax > 0, np.frexp(amax)[1] - 1 + 127 - 7, 1), 1, 254)
    scaled = (w * np.exp2(127.0 - byte)[:, None, :]).reshape(k, n).astype(np.float32)
    words = np.ascontiguousarray(scaled.reshape(k // 512, 128, 4, n).transpose(0, 1, 3, 2)).astype(ml_dtypes.float8_e4m3fn).view(np.uint8)
    return words, np.ascontiguousarray(byte.astype(np.uint8).reshape(k // 512, 16, n))


def unpack_weight(words, scales):
    g, p, n, _ = words.shape
    vals = np.ascontiguousarray(words).view(ml_dtypes.float8_e4m3fn).astype(np.float64) * np.repeat(np.exp2(scales.astype(np.float64) - 127.0), 8, axis=1)[..., None]
    return vals.transpose(0, 1, 3, 2).reshape(g * 512, n)


K, T, S, N, H = 1024, 2048, 512, 256, 512


def setup_inputs():
    n = np.random.standard_normal
    s = mx_kscale(K)[:, None]
    u = mx_kscale(H)
    packed_xT = pack_weight(n((K, T)) * s)
    return {
        "x_words": packed_xT[0],
        "x_scales": packed_xT[1],
        "w1": (n((K, H)) / np.sqrt(K) / s).astype(np.float32),
        "w2": (n((K, H)) / np.sqrt(K) / s).astype(np.float32),
        "wet": (np.random.uniform(0.2, 1.0, (H, S))).astype(np.float32),
        "npp": (np.random.uniform(0.2, 1.0, (H, S))).astype(np.float32),
        "unit": (np.random.uniform(0.6, 1.4, (H, 1)) * u[:, None]).astype(np.float32),
        "w3": (n((H, N)) / np.sqrt(H) / u[:, None]).astype(np.float32),
        "offs": striped(np.random.permutation(T)[:S]),
        "abv": striped(np.random.permutation(S)),
        "lit": striped(np.random.permutation(S)),
    }


def reference(x_words, x_scales, w1, w2, wet, npp, unit, w3, offs, abv, lit):
    xq = unpack_weight(x_words, x_scales)[:, unstriped(offs)]
    cb = mxq(f64(w1), 0, "e4m3").T @ xq
    pool_ = np.log(np.exp(cb) + 1.0)
    ca = pool_[:, unstriped(abv)]
    mixd = 0.3 * (ca - pool_)
    tm = mxq(f64(w2), 0, "e4m3").T @ xq
    q10f = np.exp(0.7 * np.tanh(tm))
    ql = q10f[:, unstriped(lit)]
    inpt = ql * f64(npp)
    resp = ((pool_ * q10f) * f64(wet)) / (pool_ + 0.8)
    hid = f64(unit) * (pool_ + mixd + 0.5 * inpt - resp)
    return mxq(f64(w3), 0, "e4m3").T @ mxq(hid, 0, "e4m3")

@@ -1,0 +1,227 @@
+from contextlib import ExitStack
+
+import concourse.mybir as mybir
+
+K, T, S, N, H = 1024, 2048, 512, 256, 512
+FLOPS = 2 * (2 * K * H * S) + 2 * H * N * S
+
+F32 = mybir.dt.float32
+BF16 = mybir.dt.bfloat16
+I32 = mybir.dt.int32
+U32 = mybir.dt.uint32
+U16 = mybir.dt.uint16
+U8 = mybir.dt.uint8
+FP8X4 = mybir.dt.float8_e4m3fn_x4
+ALU = mybir.AluOpType
+ACT = mybir.ActivationFunctionType
+
+P = 128
+PACK = 4
+PASSES = K // (P * PACK)
+CHUNKS = [256,256]
+LIT_ENGINES = ["VVVV","VSSS"]
+ABV_ENGINES = ["VVVV","SSSS"]
+SOFT_CAP = 41.0
+
+
+def tile_picked_ycarbon_bal_p_kernel(
+    tc, x_words, x_scales, w1, w2, wet, npp, unit, w3, offs, abv, lit, out
+):
+    nc = tc.nc
+    with ExitStack() as ctx:
+        sb = ctx.enter_context(tc.tile_pool(name="sb", bufs=1))
+        ps = ctx.enter_context(tc.psum_pool(name="ps", bufs=1))
+
+        def sbuf(name, shape, dtype, tag=""):
+            return sb.tile(shape, dtype, name=name, tag=tag or name, align_bytes=64)
+
+        def load_words(g):
+            words = sbuf("xw_all%d" % g, [P, T], U32)
+            nc.sync.dma_start(
+                out=words[:].bitcast(I32),
+                in_=x_words[g].rearrange("p n t -> p (n t)").bitcast(I32),
+            )
+            return words
+
+        def load_rows(name, rows):
+            raw = sbuf(name, [P, PACK, rows.shape[1]], F32)
+            nc.sync.dma_start(out=raw[:], in_=rows.rearrange("(p j) c -> p j c", j=PACK))
+            return raw
+
+        offs_t = sbuf("offs_t", [P, S // 16], U16)
+        abv_t = sbuf("abv_t", [P, S // 16], U16)
+        lit_t = sbuf("lit_t", [P, S // 16], U16)
+        xs_all = sbuf("xs_all", [P, T], U8)
+        nc.vector.memset(xs_all[:].bitcast(I32), 0)
+        nc.sync.dma_start(offs_t[:], offs)
+        xw_all = [load_words(0)]
+        for quad in range(4):
+            nc.sync.dma_start(
+                out=xs_all[32 * quad : 32 * quad + 4 * PASSES, :].bitcast(I32),
+                in_=x_scales[:, 4 * quad : 4 * quad + 4, :].bitcast(I32),
+            )
+        xw_all.append(load_words(1))
+        w2_raw = [load_rows("w2_raw%d" % g, w2[512 * g : 512 * (g + 1), :]) for g in range(PASSES)]
+        w1_raw = [load_rows("w1_raw%d" % g, w1[512 * g : 512 * (g + 1), :]) for g in range(PASSES)]
+        nc.sync.dma_start(lit_t[:], lit)
+        unit_sb = sbuf("unit_sb", [P, PACK], F32)
+        nc.sync.dma_start(out=unit_sb[:], in_=unit.rearrange("(p j) c -> p (j c)", j=PACK))
+        nc.sync.dma_start(abv_t[:], abv)
+        npp_sb = load_rows("npp_sb", npp)
+        wet_sb = load_rows("wet_sb", wet)
+        w3_raw = load_rows("w3_raw", w3)
+
+        xw = [sbuf("xw%d" % g, [P, S], U32) for g in range(PASSES)]
+        xs = sbuf("xs", [P, S], U8)
+        nc.vector.tensor_copy(xw[0][:], xw_all[0][:].indirect(offs_t[:]))
+        nc.vector.tensor_copy(xs[:], xs_all[:].indirect(offs_t[:]))
+        nc.vector.tensor_copy(xw[1][:], xw_all[1][:].indirect(offs_t[:]))
+
+        def quantise_dealt(name, raw, vector_m, pieces):
+            grouped = sbuf(name + "_bf", [P, PACK, P, PACK], BF16)
+            src = raw[:].rearrange("p j (m t) -> p m j t", t=PACK)
+            dst = grouped[:].rearrange("p t m j -> p m j t")
+            if vector_m > 0:
+                nc.vector.tensor_copy(dst[:, :vector_m], src[:, :vector_m])
+            if vector_m < P:
+                nc.scalar.copy(dst[:, vector_m:], src[:, vector_m:])
+            codes = sbuf(name + "_codes", [P, H], U32)
+            scales = sbuf(name + "_scales", [P, H], U8)
+            flat = grouped[:].rearrange("p t m j -> p (t m j)")
+            step = H // pieces
+            for c0 in range(0, H, step):
+                nc.vector.quantize_mx(
+                    out=codes[:, c0 : c0 + step].bitcast(FP8X4),
+                    scales=scales[:, c0 : c0 + step],
+                    in_=flat[:, PACK * c0 : PACK * (c0 + step)],
+                )
+            return codes, scales
+
+        def product(bank, quantised, t):
+            for g in range(PASSES):
+                codes, scales = quantised[g]
+                nc.tensor.matmul_mx(
+                    out=bank[:],
+                    lhsT=codes[:, P * t : P * (t + 1)].bitcast(FP8X4),
+                    lhsT_scale=scales[:, P * t : P * (t + 1)],
+                    rhs=xw[g][:].bitcast(FP8X4),
+                    rhs_scale=xs[4 * g :, :],
+                    start=(g == 0),
+                    stop=(g == PASSES - 1),
+                )
+
+        def gather(engine, dst, window, entries):
+            if engine == "V":
+                nc.vector.tensor_copy(dst, window.indirect(entries))
+            else:
+                nc.scalar.activation(dst, window.indirect(entries), ACT.Copy)
+
+        w2_q = [quantise_dealt("w2_0", w2_raw[0], 128, 1), quantise_dealt("w2_1", w2_raw[1], 88, 2)]
+        th = sbuf("th", [P, PACK, S], F32)
+        q = []
+        for t in range(PACK):
+            tm = ps.tile([P, S], F32, name="tm%d" % t, tag="bank%d" % t)
+            product(tm, w2_q, t)
+            nc.scalar.activation(th[:, t, :], tm[:], ACT.Tanh)
+            q_t = sbuf("q%d" % t, [P, S], F32)
+            nc.scalar.activation(q_t[:], th[:, t, :], ACT.Exp, scale=0.7)
+            q.append(q_t)
+
+        w1_q = [quantise_dealt("w1_0", w1_raw[0], 128, 1), quantise_dealt("w1_1", w1_raw[1], 128, 2)]
+        grown = sbuf("grown", [P, PACK, S], F32)
+        soft = sbuf("soft", [P, PACK, S], F32)
+        cb = []
+        for t in range(PACK):
+            bank = ps.tile([P, S], F32, name="cb%d" % t, tag="bank%d" % (PACK + t))
+            product(bank, w1_q, t)
+            nc.scalar.activation(grown[:, t, :], bank[:], ACT.Exp)
+            cb.append(bank)
+        pool = [sbuf("pool%d" % t, [P, S], F32) for t in range(PACK)]
+        halves = [slice(0, S // 2), slice(S // 2, S)]
+        for cols in halves:
+            nc.scalar.activation(soft[:, :, cols], grown[:, :, cols], ACT.Ln, bias=1.0)
+        for cols in halves:
+            for t in range(PACK):
+                nc.vector.scalar_tensor_tensor(
+                    pool[t][:, cols], soft[:, t, cols], SOFT_CAP, cb[t][:, cols], ALU.min, ALU.max
+                )
+        sat = sbuf("sat", [P, PACK, S], F32)
+        for t in range(PACK):
+            nc.scalar.activation(sat[:, t, :], pool[t][:], ACT.Ln, scale=1.25, bias=1.0)
+        starts = [sum(CHUNKS[:c]) for c in range(len(CHUNKS))]
+        for c, width in enumerate(CHUNKS):
+            cols = slice(starts[c], starts[c] + width)
+            nc.scalar.activation(sat[:, :, cols], sat[:, :, cols], ACT.Exp, scale=-1.0)
+
+        u_resp = sbuf("u_resp", [P, PACK], F32)
+        u_keep = sbuf("u_keep", [P, PACK], F32)
+        u_mix = sbuf("u_mix", [P, PACK], F32)
+        u_lit = sbuf("u_lit", [P, PACK], F32)
+        for dst, factor in ((u_resp, -1.25), (u_keep, 0.7), (u_mix, 0.3), (u_lit, 0.5)):
+            nc.vector.tensor_scalar(dst[:], unit_sb[:], factor, 0.0, ALU.mult, ALU.add)
+
+        w3_bf = sbuf("w3_bf", [P, N, PACK], BF16, tag="grown")
+        w3_codes = sbuf("w3_codes", [P, N], U32)
+        w3_scales = sbuf("w3_scales", [P, N], U8)
+
+        for c, width in enumerate(CHUNKS):
+            cols = slice(starts[c], starts[c] + width)
+            entries = slice(starts[c] // 16, (starts[c] + width) // 16)
+            litter = sbuf("litter%d" % c, [P, PACK, width], F32)
+            moved = sbuf("moved%d" % c, [P, PACK, width], F32)
+            own = sbuf("own%d" % c, [P, PACK, width], F32)
+            for t in range(PACK):
+                gather(ABV_ENGINES[c][t], moved[:, t, :], pool[t][:], abv_t[:, entries])
+            for t in range(PACK):
+                gather(LIT_ENGINES[c][t], litter[:, t, :], q[t][:], lit_t[:, entries])
+            for t in range(PACK):
+                nc.vector.scalar_tensor_tensor(
+                    own[:, t, :], q[t][:, cols], u_resp[:, t : t + 1], wet_sb[:, t, cols], ALU.mult, ALU.mult
+                )
+            nc.vector.tensor_tensor(own[:], own[:], sat[:, :, cols], ALU.mult)
+            for t in range(PACK):
+                nc.vector.scalar_tensor_tensor(
+                    litter[:, t, :], litter[:, t, :], u_lit[:, t : t + 1], npp_sb[:, t, cols], ALU.mult, ALU.mult
+                )
+            for t in range(PACK):
+                nc.vector.scalar_tensor_tensor(
+                    own[:, t, :], own[:, t, :], u_keep[:, t : t + 1], pool[t][:, cols], ALU.add, ALU.mult
+                )
+            for t in range(PACK):
+                nc.vector.scalar_tensor_tensor(
+                    moved[:, t, :], moved[:, t, :], u_mix[:, t : t + 1], litter[:, t, :], ALU.mult, ALU.add
+                )
+            if c == 0:
+                nc.scalar.copy(
+                    w3_bf[:].rearrange("p (c i) j -> p c j i", i=4),
+                    w3_raw[:].rearrange("p j (c i) -> p c j i", i=4),
+                )
+                nc.vector.quantize_mx(
+                    out=w3_codes[:].bitcast(FP8X4), scales=w3_scales[:], in_=w3_bf[:].rearrange("p n j -> p (n j)")
+                )
+            hid = sbuf("hid%d" % c, [P, width, PACK], BF16)
+            nc.vector.tensor_tensor(
+                hid[:].rearrange("p (c i) t -> p c t i", i=4),
+                own[:].rearrange("p t (c i) -> p c t i", i=4),
+                moved[:].rearrange("p t (c i) -> p c t i", i=4),
+                ALU.add,
+            )
+            hid_codes = sbuf("hid_codes%d" % c, [P, width], U32)
+            hid_scales = sbuf("hid_scales%d" % c, [P, width], U8)
+            nc.vector.quantize_mx(
+                out=hid_codes[:].bitcast(FP8X4), scales=hid_scales[:], in_=hid[:].rearrange("p n t -> p (n t)")
+            )
+            flux = ps.tile([P, N // P, width], F32, name="flux%d" % c, tag="bank%d" % c)
+            for b in range(N // P):
+                nc.tensor.matmul_mx(
+                    out=flux[:, b, :],
+                    lhsT=w3_codes[:, P * b : P * (b + 1)].bitcast(FP8X4),
+                    lhsT_scale=w3_scales[:, P * b : P * (b + 1)],
+                    rhs=hid_codes[:].bitcast(FP8X4),
+                    rhs_scale=hid_scales[:],
+                    start=True,
+                    stop=True,
+                )
+            flux_sb = sbuf("flux_sb%d" % c, [P, N // P, width], F32)
+            nc.scalar.copy(flux_sb[:], flux[:])
+            nc.sync.dma_start(out=out[:, cols].rearrange("(b p) j -> p b j", p=P), in_=flux_sb[:])

@@ -19,8 +19,8 @@ P = 128
 PACK = 4
 PASSES = K // (P * PACK)
 CHUNKS = [256,256]
-LIT_ENGINES = ["VVVV","VSSS"]
-ABV_ENGINES = ["VVVV","SSSS"]
+LIT_ENGINES = "VS"
+ABV_ENGINES = "VS"
 SOFT_CAP = 41.0
 
 
@@ -54,22 +54,25 @@ def tile_picked_ycarbon_bal_p_kernel(
         xs_all = sbuf("xs_all", [P, T], U8)
         nc.vector.memset(xs_all[:].bitcast(I32), 0)
         nc.sync.dma_start(offs_t[:], offs)
-        xw_all = [load_words(0)]
+        w2_raw0 = load_rows("w2_raw0", w2[:512, :])
         for quad in range(4):
             nc.sync.dma_start(
                 out=xs_all[32 * quad : 32 * quad + 4 * PASSES, :].bitcast(I32),
                 in_=x_scales[:, 4 * quad : 4 * quad + 4, :].bitcast(I32),
             )
-        xw_all.append(load_words(1))
-        w2_raw = [load_rows("w2_raw%d" % g, w2[512 * g : 512 * (g + 1), :]) for g in range(PASSES)]
-        w1_raw = [load_rows("w1_raw%d" % g, w1[512 * g : 512 * (g + 1), :]) for g in range(PASSES)]
-        nc.sync.dma_start(lit_t[:], lit)
+        xw_all0 = load_words(0)
+        w2_raw1 = load_rows("w2_raw1", w2[512:, :])
+        xw_all1 = load_words(1)
         unit_sb = sbuf("unit_sb", [P, PACK], F32)
         nc.sync.dma_start(out=unit_sb[:], in_=unit.rearrange("(p j) c -> p (j c)", j=PACK))
+        w1_raw0 = load_rows("w1_raw0", w1[:512, :])
+        w1_raw1 = load_rows("w1_raw1", w1[512:, :])
         nc.sync.dma_start(abv_t[:], abv)
         npp_sb = load_rows("npp_sb", npp)
+        nc.sync.dma_start(lit_t[:], lit)
         wet_sb = load_rows("wet_sb", wet)
         w3_raw = load_rows("w3_raw", w3)
+        xw_all = [xw_all0, xw_all1]
 
         xw = [sbuf("xw%d" % g, [P, S], U32) for g in range(PASSES)]
         xs = sbuf("xs", [P, S], U8)
@@ -116,7 +119,14 @@ def tile_picked_ycarbon_bal_p_kernel(
             else:
                 nc.scalar.activation(dst, window.indirect(entries), ACT.Copy)
 
-        w2_q = [quantise_dealt("w2_0", w2_raw[0], 128, 1), quantise_dealt("w2_1", w2_raw[1], 88, 2)]
+        u_resp = sbuf("u_resp", [P, PACK], F32)
+        u_keep = sbuf("u_keep", [P, PACK], F32)
+        u_mix = sbuf("u_mix", [P, PACK], F32)
+        u_lit = sbuf("u_lit", [P, PACK], F32)
+
+        w2_q = [quantise_dealt("w2_0", w2_raw0, 0, 1), quantise_dealt("w2_1", w2_raw1, 48, 1)]
+        for dst, factor in ((u_resp, -1.25), (u_keep, 0.7), (u_mix, 0.3), (u_lit, 0.5)):
+            nc.vector.tensor_scalar(dst[:], unit_sb[:], factor, 0.0, ALU.mult, ALU.add)
         th = sbuf("th", [P, PACK, S], F32)
         q = []
         for t in range(PACK):
@@ -127,91 +137,54 @@ def tile_picked_ycarbon_bal_p_kernel(
             nc.scalar.activation(q_t[:], th[:, t, :], ACT.Exp, scale=0.7)
             q.append(q_t)
 
-        w1_q = [quantise_dealt("w1_0", w1_raw[0], 128, 1), quantise_dealt("w1_1", w1_raw[1], 128, 2)]
-        grown = sbuf("grown", [P, PACK, S], F32)
+        w1_q = [quantise_dealt("w1_0", w1_raw0, 128, 1), quantise_dealt("w1_1", w1_raw1, 128, 2)]
         soft = sbuf("soft", [P, PACK, S], F32)
         cb = []
         for t in range(PACK):
             bank = ps.tile([P, S], F32, name="cb%d" % t, tag="bank%d" % (PACK + t))
             product(bank, w1_q, t)
-            nc.scalar.activation(grown[:, t, :], bank[:], ACT.Exp)
+            nc.scalar.activation(soft[:, t, :], bank[:], ACT.Exp)
             cb.append(bank)
-        pool = [sbuf("pool%d" % t, [P, S], F32) for t in range(PACK)]
-        halves = [slice(0, S // 2), slice(S // 2, S)]
-        for cols in halves:
-            nc.scalar.activation(soft[:, :, cols], grown[:, :, cols], ACT.Ln, bias=1.0)
-        for cols in halves:
-            for t in range(PACK):
-                nc.vector.scalar_tensor_tensor(
-                    pool[t][:, cols], soft[:, t, cols], SOFT_CAP, cb[t][:, cols], ALU.min, ALU.max
-                )
-        sat = sbuf("sat", [P, PACK, S], F32)
         for t in range(PACK):
-            nc.scalar.activation(sat[:, t, :], pool[t][:], ACT.Ln, scale=1.25, bias=1.0)
+            nc.scalar.activation(soft[:, t, :], soft[:, t, :], ACT.Ln, bias=1.0)
+        pool = [sbuf("pool%d" % t, [P, S], F32) for t in range(PACK)]
+        for t in range(PACK):
+            nc.vector.scalar_tensor_tensor(pool[t][:], soft[:, t, :], SOFT_CAP, cb[t][:], ALU.min, ALU.max)
+        log_sum = sbuf("log_sum", [P, PACK, S], F32)
+        for t in range(PACK):
+            nc.scalar.activation(log_sum[:, t, :], pool[t][:], ACT.Ln, scale=1.25, bias=1.0)
+        sat = sbuf("sat", [P, PACK, S], F32)
         starts = [sum(CHUNKS[:c]) for c in range(len(CHUNKS))]
         for c, width in enumerate(CHUNKS):
-            cols = slice(starts[c], starts[c] + width)
-            nc.scalar.activation(sat[:, :, cols], sat[:, :, cols], ACT.Exp, scale=-1.0)
+            first = sum(CHUNKS[:c])
+            cols = slice(first, first + width)
+            nc.scalar.activation(sat[:, :, cols], log_sum[:, :, cols], ACT.Exp, scale=-1.0)
 
-        u_resp = sbuf("u_resp", [P, PACK], F32)
-        u_keep = sbuf("u_keep", [P, PACK], F32)
-        u_mix = sbuf("u_mix", [P, PACK], F32)
-        u_lit = sbuf("u_lit", [P, PACK], F32)
-        for dst, factor in ((u_resp, -1.25), (u_keep, 0.7), (u_mix, 0.3), (u_lit, 0.5)):
-            nc.vector.tensor_scalar(dst[:], unit_sb[:], factor, 0.0, ALU.mult, ALU.add)
+        own = sbuf("own", [P, PACK, S], F32)
+        for t in range(PACK):
+            nc.vector.scalar_tensor_tensor(own[:, t, :], q[t][:], u_resp[:, t : t + 1], wet_sb[:, t, :], ALU.mult, ALU.mult)
 
-        w3_bf = sbuf("w3_bf", [P, N, PACK], BF16, tag="grown")
+
         w3_codes = sbuf("w3_codes", [P, N], U32)
         w3_scales = sbuf("w3_scales", [P, N], U8)
-
-        for c, width in enumerate(CHUNKS):
-            cols = slice(starts[c], starts[c] + width)
-            entries = slice(starts[c] // 16, (starts[c] + width) // 16)
-            litter = sbuf("litter%d" % c, [P, PACK, width], F32)
-            moved = sbuf("moved%d" % c, [P, PACK, width], F32)
-            own = sbuf("own%d" % c, [P, PACK, width], F32)
-            for t in range(PACK):
-                gather(ABV_ENGINES[c][t], moved[:, t, :], pool[t][:], abv_t[:, entries])
-            for t in range(PACK):
-                gather(LIT_ENGINES[c][t], litter[:, t, :], q[t][:], lit_t[:, entries])
-            for t in range(PACK):
-                nc.vector.scalar_tensor_tensor(
-                    own[:, t, :], q[t][:, cols], u_resp[:, t : t + 1], wet_sb[:, t, cols], ALU.mult, ALU.mult
-                )
-            nc.vector.tensor_tensor(own[:], own[:], sat[:, :, cols], ALU.mult)
-            for t in range(PACK):
-                nc.vector.scalar_tensor_tensor(
-                    litter[:, t, :], litter[:, t, :], u_lit[:, t : t + 1], npp_sb[:, t, cols], ALU.mult, ALU.mult
-                )
-            for t in range(PACK):
-                nc.vector.scalar_tensor_tensor(
-                    own[:, t, :], own[:, t, :], u_keep[:, t : t + 1], pool[t][:, cols], ALU.add, ALU.mult
-                )
-            for t in range(PACK):
-                nc.vector.scalar_tensor_tensor(
-                    moved[:, t, :], moved[:, t, :], u_mix[:, t : t + 1], litter[:, t, :], ALU.mult, ALU.add
-                )
-            if c == 0:
-                nc.scalar.copy(
-                    w3_bf[:].rearrange("p (c i) j -> p c j i", i=4),
-                    w3_raw[:].rearrange("p j (c i) -> p c j i", i=4),
-                )
-                nc.vector.quantize_mx(
-                    out=w3_codes[:].bitcast(FP8X4), scales=w3_scales[:], in_=w3_bf[:].rearrange("p n j -> p (n j)")
-                )
-            hid = sbuf("hid%d" % c, [P, width, PACK], BF16)
+        late = sbuf("late", [P, PACK * S + PACK * N // 2], F32, tag="log_sum")
+        w3_bf = late[:, PACK * S :].bitcast(BF16).rearrange("p (n j) -> p n j", j=PACK)
+        def finish(kept, gained, first):
+            width = kept.shape[2]
+            name = "%d" % first
+            hid = sbuf("hid" + name, [P, width, PACK], BF16)
             nc.vector.tensor_tensor(
                 hid[:].rearrange("p (c i) t -> p c t i", i=4),
-                own[:].rearrange("p t (c i) -> p c t i", i=4),
-                moved[:].rearrange("p t (c i) -> p c t i", i=4),
+                kept.rearrange("p t (c i) -> p c t i", i=4),
+                gained.rearrange("p t (c i) -> p c t i", i=4),
                 ALU.add,
             )
-            hid_codes = sbuf("hid_codes%d" % c, [P, width], U32)
-            hid_scales = sbuf("hid_scales%d" % c, [P, width], U8)
+            hid_codes = sbuf("hid_codes" + name, [P, width], U32)
+            hid_scales = sbuf("hid_scales" + name, [P, width], U8)
             nc.vector.quantize_mx(
                 out=hid_codes[:].bitcast(FP8X4), scales=hid_scales[:], in_=hid[:].rearrange("p n t -> p (n t)")
             )
-            flux = ps.tile([P, N // P, width], F32, name="flux%d" % c, tag="bank%d" % c)
+            flux = ps.tile([P, N // P, width], F32, name="flux" + name, tag="bank%d" % (first // P))
             for b in range(N // P):
                 nc.tensor.matmul_mx(
                     out=flux[:, b, :],
@@ -222,6 +195,48 @@ def tile_picked_ycarbon_bal_p_kernel(
                     start=True,
                     stop=True,
                 )
-            flux_sb = sbuf("flux_sb%d" % c, [P, N // P, width], F32)
+            flux_sb = sbuf("flux_sb" + name, [P, N // P, width], F32)
             nc.scalar.copy(flux_sb[:], flux[:])
-            nc.sync.dma_start(out=out[:, cols].rearrange("(b p) j -> p b j", p=P), in_=flux_sb[:])
+            nc.sync.dma_start(out=out[:, first : first + width].rearrange("(b p) j -> p b j", p=P), in_=flux_sb[:])
+
+        used = 0
+        for c, width in enumerate(CHUNKS):
+            cols = slice(starts[c], starts[c] + width)
+            entries = slice(starts[c] // 16, (starts[c] + width) // 16)
+            fetched = []
+            for name, engine in (("litter", LIT_ENGINES[c]), ("moved", ABV_ENGINES[c])):
+                if engine == "S":
+                    fetched.append(late[:, used : used + PACK * width].rearrange("p (t j) -> p t j", t=PACK))
+                    used = used + PACK * width
+                else:
+                    fetched.append(sbuf("%s%d" % (name, c), [P, PACK, width], F32)[:])
+            litter, moved = fetched
+            nc.vector.tensor_tensor(own[:, :, cols], own[:, :, cols], sat[:, :, cols], ALU.mult)
+            for t in range(PACK):
+                nc.vector.scalar_tensor_tensor(
+                    own[:, t, cols], own[:, t, cols], u_keep[:, t : t + 1], pool[t][:, cols], ALU.add, ALU.mult
+                )
+            if c == 0:
+                nc.scalar.copy(
+                    w3_bf.rearrange("p (c i) j -> p c j i", i=4),
+                    w3_raw[:].rearrange("p j (c i) -> p c j i", i=4),
+                )
+                nc.vector.quantize_mx(
+                    out=w3_codes[:].bitcast(FP8X4), scales=w3_scales[:], in_=w3_bf.rearrange("p n j -> p (n j)")
+                )
+            for t in range(PACK):
+                gather(LIT_ENGINES[c], litter[:, t, :], q[t][:], lit_t[:, entries])
+            for t in range(PACK):
+                gather(ABV_ENGINES[c], moved[:, t, :], pool[t][:], abv_t[:, entries])
+            for t in range(PACK):
+                nc.vector.scalar_tensor_tensor(
+                    litter[:, t, :], litter[:, t, :], u_lit[:, t : t + 1], npp_sb[:, t, cols], ALU.mult, ALU.mult
+                )
+            for t in range(PACK):
+                nc.vector.scalar_tensor_tensor(
+                    moved[:, t, :], moved[:, t, :], u_mix[:, t : t + 1], litter[:, t, :], ALU.mult, ALU.add
+                )
+            done = 0
+            for piece in [[256], [128, 128]][c]:
+                finish(own[:, :, starts[c] + done : starts[c] + done + piece], moved[:, :, done : done + piece], starts[c] + done)
+                done = done + piece

from contextlib import ExitStack

import concourse.mybir as mybir

K, T, S, N, H = 1024, 2048, 512, 256, 512
FLOPS = 2 * (2 * K * H * S) + 2 * H * N * S

F32 = mybir.dt.float32
BF16 = mybir.dt.bfloat16
I32 = mybir.dt.int32
U32 = mybir.dt.uint32
U16 = mybir.dt.uint16
U8 = mybir.dt.uint8
FP8X4 = mybir.dt.float8_e4m3fn_x4
ALU = mybir.AluOpType
ACT = mybir.ActivationFunctionType

P = 128
PACK = 4
PASSES = K // (P * PACK)
CHUNKS = [256,256]
LIT_ENGINES = "VS"
ABV_ENGINES = "VS"
SOFT_CAP = 41.0


def tile_picked_ycarbon_bal_p_kernel(
    tc, x_words, x_scales, w1, w2, wet, npp, unit, w3, offs, abv, lit, out
):
    nc = tc.nc
    with ExitStack() as ctx:
        sb = ctx.enter_context(tc.tile_pool(name="sb", bufs=1))
        ps = ctx.enter_context(tc.psum_pool(name="ps", bufs=1))

        def sbuf(name, shape, dtype, tag=""):
            return sb.tile(shape, dtype, name=name, tag=tag or name, align_bytes=64)

        def load_words(g):
            words = sbuf("xw_all%d" % g, [P, T], U32)
            nc.sync.dma_start(
                out=words[:].bitcast(I32),
                in_=x_words[g].rearrange("p n t -> p (n t)").bitcast(I32),
            )
            return words

        def load_rows(name, rows):
            raw = sbuf(name, [P, PACK, rows.shape[1]], F32)
            nc.sync.dma_start(out=raw[:], in_=rows.rearrange("(p j) c -> p j c", j=PACK))
            return raw

        offs_t = sbuf("offs_t", [P, S // 16], U16)
        abv_t = sbuf("abv_t", [P, S // 16], U16)
        lit_t = sbuf("lit_t", [P, S // 16], U16)
        xs_all = sbuf("xs_all", [P, T], U8)
        nc.vector.memset(xs_all[:].bitcast(I32), 0)
        nc.sync.dma_start(offs_t[:], offs)
        w2_raw0 = load_rows("w2_raw0", w2[:512, :])
        for quad in range(4):
            nc.sync.dma_start(
                out=xs_all[32 * quad : 32 * quad + 4 * PASSES, :].bitcast(I32),
                in_=x_scales[:, 4 * quad : 4 * quad + 4, :].bitcast(I32),
            )
        xw_all0 = load_words(0)
        w2_raw1 = load_rows("w2_raw1", w2[512:, :])
        xw_all1 = load_words(1)
        unit_sb = sbuf("unit_sb", [P, PACK], F32)
        nc.sync.dma_start(out=unit_sb[:], in_=unit.rearrange("(p j) c -> p (j c)", j=PACK))
        w1_raw0 = load_rows("w1_raw0", w1[:512, :])
        w1_raw1 = load_rows("w1_raw1", w1[512:, :])
        nc.sync.dma_start(abv_t[:], abv)
        npp_sb = load_rows("npp_sb", npp)
        nc.sync.dma_start(lit_t[:], lit)
        wet_sb = load_rows("wet_sb", wet)
        w3_raw = load_rows("w3_raw", w3)
        xw_all = [xw_all0, xw_all1]

        xw = [sbuf("xw%d" % g, [P, S], U32) for g in range(PASSES)]
        xs = sbuf("xs", [P, S], U8)
        nc.vector.tensor_copy(xw[0][:], xw_all[0][:].indirect(offs_t[:]))
        nc.vector.tensor_copy(xs[:], xs_all[:].indirect(offs_t[:]))
        nc.vector.tensor_copy(xw[1][:], xw_all[1][:].indirect(offs_t[:]))

        def quantise_dealt(name, raw, vector_m, pieces):
            grouped = sbuf(name + "_bf", [P, PACK, P, PACK], BF16)
            src = raw[:].rearrange("p j (m t) -> p m j t", t=PACK)
            dst = grouped[:].rearrange("p t m j -> p m j t")
            if vector_m > 0:
                nc.vector.tensor_copy(dst[:, :vector_m], src[:, :vector_m])
            if vector_m < P:
                nc.scalar.copy(dst[:, vector_m:], src[:, vector_m:])
            codes = sbuf(name + "_codes", [P, H], U32)
            scales = sbuf(name + "_scales", [P, H], U8)
            flat = grouped[:].rearrange("p t m j -> p (t m j)")
            step = H // pieces
            for c0 in range(0, H, step):
                nc.vector.quantize_mx(
                    out=codes[:, c0 : c0 + step].bitcast(FP8X4),
                    scales=scales[:, c0 : c0 + step],
                    in_=flat[:, PACK * c0 : PACK * (c0 + step)],
                )
            return codes, scales

        def product(bank, quantised, t):
            for g in range(PASSES):
                codes, scales = quantised[g]
                nc.tensor.matmul_mx(
                    out=bank[:],
                    lhsT=codes[:, P * t : P * (t + 1)].bitcast(FP8X4),
                    lhsT_scale=scales[:, P * t : P * (t + 1)],
                    rhs=xw[g][:].bitcast(FP8X4),
                    rhs_scale=xs[4 * g :, :],
                    start=(g == 0),
                    stop=(g == PASSES - 1),
                )

        def gather(engine, dst, window, entries):
            if engine == "V":
                nc.vector.tensor_copy(dst, window.indirect(entries))
            else:
                nc.scalar.activation(dst, window.indirect(entries), ACT.Copy)

        u_resp = sbuf("u_resp", [P, PACK], F32)
        u_keep = sbuf("u_keep", [P, PACK], F32)
        u_mix = sbuf("u_mix", [P, PACK], F32)
        u_lit = sbuf("u_lit", [P, PACK], F32)

        w2_q = [quantise_dealt("w2_0", w2_raw0, 0, 1), quantise_dealt("w2_1", w2_raw1, 48, 1)]
        for dst, factor in ((u_resp, -1.25), (u_keep, 0.7), (u_mix, 0.3), (u_lit, 0.5)):
            nc.vector.tensor_scalar(dst[:], unit_sb[:], factor, 0.0, ALU.mult, ALU.add)
        th = sbuf("th", [P, PACK, S], F32)
        q = []
        for t in range(PACK):
            tm = ps.tile([P, S], F32, name="tm%d" % t, tag="bank%d" % t)
            product(tm, w2_q, t)
            nc.scalar.activation(th[:, t, :], tm[:], ACT.Tanh)
            q_t = sbuf("q%d" % t, [P, S], F32)
            nc.scalar.activation(q_t[:], th[:, t, :], ACT.Exp, scale=0.7)
            q.append(q_t)

        w1_q = [quantise_dealt("w1_0", w1_raw0, 128, 1), quantise_dealt("w1_1", w1_raw1, 128, 2)]
        soft = sbuf("soft", [P, PACK, S], F32)
        cb = []
        for t in range(PACK):
            bank = ps.tile([P, S], F32, name="cb%d" % t, tag="bank%d" % (PACK + t))
            product(bank, w1_q, t)
            nc.scalar.activation(soft[:, t, :], bank[:], ACT.Exp)
            cb.append(bank)
        for t in range(PACK):
            nc.scalar.activation(soft[:, t, :], soft[:, t, :], ACT.Ln, bias=1.0)
        pool = [sbuf("pool%d" % t, [P, S], F32) for t in range(PACK)]
        for t in range(PACK):
            nc.vector.scalar_tensor_tensor(pool[t][:], soft[:, t, :], SOFT_CAP, cb[t][:], ALU.min, ALU.max)
        log_sum = sbuf("log_sum", [P, PACK, S], F32)
        for t in range(PACK):
            nc.scalar.activation(log_sum[:, t, :], pool[t][:], ACT.Ln, scale=1.25, bias=1.0)
        sat = sbuf("sat", [P, PACK, S], F32)
        starts = [sum(CHUNKS[:c]) for c in range(len(CHUNKS))]
        for c, width in enumerate(CHUNKS):
            first = sum(CHUNKS[:c])
            cols = slice(first, first + width)
            nc.scalar.activation(sat[:, :, cols], log_sum[:, :, cols], ACT.Exp, scale=-1.0)

        own = sbuf("own", [P, PACK, S], F32)
        for t in range(PACK):
            nc.vector.scalar_tensor_tensor(own[:, t, :], q[t][:], u_resp[:, t : t + 1], wet_sb[:, t, :], ALU.mult, ALU.mult)


        w3_codes = sbuf("w3_codes", [P, N], U32)
        w3_scales = sbuf("w3_scales", [P, N], U8)
        late = sbuf("late", [P, PACK * S + PACK * N // 2], F32, tag="log_sum")
        w3_bf = late[:, PACK * S :].bitcast(BF16).rearrange("p (n j) -> p n j", j=PACK)
        def finish(kept, gained, first):
            width = kept.shape[2]
            name = "%d" % first
            hid = sbuf("hid" + name, [P, width, PACK], BF16)
            nc.vector.tensor_tensor(
                hid[:].rearrange("p (c i) t -> p c t i", i=4),
                kept.rearrange("p t (c i) -> p c t i", i=4),
                gained.rearrange("p t (c i) -> p c t i", i=4),
                ALU.add,
            )
            hid_codes = sbuf("hid_codes" + name, [P, width], U32)
            hid_scales = sbuf("hid_scales" + name, [P, width], U8)
            nc.vector.quantize_mx(
                out=hid_codes[:].bitcast(FP8X4), scales=hid_scales[:], in_=hid[:].rearrange("p n t -> p (n t)")
            )
            flux = ps.tile([P, N // P, width], F32, name="flux" + name, tag="bank%d" % (first // P))
            for b in range(N // P):
                nc.tensor.matmul_mx(
                    out=flux[:, b, :],
                    lhsT=w3_codes[:, P * b : P * (b + 1)].bitcast(FP8X4),
                    lhsT_scale=w3_scales[:, P * b : P * (b + 1)],
                    rhs=hid_codes[:].bitcast(FP8X4),
                    rhs_scale=hid_scales[:],
                    start=True,
                    stop=True,
                )
            flux_sb = sbuf("flux_sb" + name, [P, N // P, width], F32)
            nc.scalar.copy(flux_sb[:], flux[:])
            nc.sync.dma_start(out=out[:, first : first + width].rearrange("(b p) j -> p b j", p=P), in_=flux_sb[:])

        used = 0
        for c, width in enumerate(CHUNKS):
            cols = slice(starts[c], starts[c] + width)
            entries = slice(starts[c] // 16, (starts[c] + width) // 16)
            fetched = []
            for name, engine in (("litter", LIT_ENGINES[c]), ("moved", ABV_ENGINES[c])):
                if engine == "S":
                    fetched.append(late[:, used : used + PACK * width].rearrange("p (t j) -> p t j", t=PACK))
                    used = used + PACK * width
                else:
                    fetched.append(sbuf("%s%d" % (name, c), [P, PACK, width], F32)[:])
            litter, moved = fetched
            nc.vector.tensor_tensor(own[:, :, cols], own[:, :, cols], sat[:, :, cols], ALU.mult)
            for t in range(PACK):
                nc.vector.scalar_tensor_tensor(
                    own[:, t, cols], own[:, t, cols], u_keep[:, t : t + 1], pool[t][:, cols], ALU.add, ALU.mult
                )
            if c == 0:
                nc.scalar.copy(
                    w3_bf.rearrange("p (c i) j -> p c j i", i=4),
                    w3_raw[:].rearrange("p j (c i) -> p c j i", i=4),
                )
                nc.vector.quantize_mx(
                    out=w3_codes[:].bitcast(FP8X4), scales=w3_scales[:], in_=w3_bf.rearrange("p n j -> p (n j)")
                )
            for t in range(PACK):
                gather(LIT_ENGINES[c], litter[:, t, :], q[t][:], lit_t[:, entries])
            for t in range(PACK):
                gather(ABV_ENGINES[c], moved[:, t, :], pool[t][:], abv_t[:, entries])
            for t in range(PACK):
                nc.vector.scalar_tensor_tensor(
                    litter[:, t, :], litter[:, t, :], u_lit[:, t : t + 1], npp_sb[:, t, cols], ALU.mult, ALU.mult
                )
            for t in range(PACK):
                nc.vector.scalar_tensor_tensor(
                    moved[:, t, :], moved[:, t, :], u_mix[:, t : t + 1], litter[:, t, :], ALU.mult, ALU.add
                )
            done = 0
            for piece in [[256], [128, 128]][c]:
                finish(own[:, :, starts[c] + done : starts[c] + done + piece], moved[:, :, done : done + piece], starts[c] + done)
                done = done + piece
